import numpy as np
import ml_dtypes


def mxq(x, axis, fmt="e4m3"):
    dtype, down = {"e4m3": (ml_dtypes.float8_e4m3fn, 7), "e5m2": (ml_dtypes.float8_e5m2, 14)}[fmt]
    v = np.moveaxis(np.asarray(x, np.float32).astype(ml_dtypes.bfloat16).astype(np.float64), axis, -1)
    blocks = v.reshape(v.shape[:-1] + (-1, 32))
    amax = np.abs(blocks).max(-1, keepdims=True)
    byte = np.maximum(np.where(amax > 0, np.frexp(amax)[1] - 1 + 127, 0) - down, 1)
    scale = np.exp2(byte - 127.0)
    codes = (blocks / scale).astype(np.float32).astype(dtype).astype(np.float64)
    return np.moveaxis((codes * scale).reshape(v.shape), -1, axis)


WIDE = False


def mx_kscale(k):
    if not WIDE:
        return np.ones(k)
    levels = np.array([10, -10, 5, -5, 0])
    if k % 512:
        return np.exp2(np.random.permutation(np.resize(levels, k // 32))).repeat(32)
    a = np.empty((k // 512, 16))
    for p in range(k // 512):
        a[p, :8] = np.random.permutation(np.resize(levels, 8))
        for g in range(8):
            far = levels[np.abs(levels - a[p, g]) >= 10]
            a[p, g + 8] = far[np.random.randint(len(far))]
    return np.exp2(a.ravel()).repeat(32)


def f64(x):
    return np.asarray(x).astype(np.float64)


def striped(idx):
    return np.tile(idx.reshape(-1, 16).T, (8, 1)).astype(np.uint16)


def unstriped(offs):
    return offs[:16].T.reshape(-1).astype(np.int64)


def striped8(idx):
    return np.concatenate([x.reshape(-1, 16).T for x in idx]).astype(np.uint16)


def runs(offs, k):
    lists = np.stack([offs[16 * r : 16 * r + 16].T.reshape(-1) for r in range(8)]).astype(np.int64)
    return lists[np.arange(k) % 512 // 64]


def pack_weight(w):
    k, n = w.shape
    w = f64(np.asarray(w, np.float32).astype(ml_dtypes.bfloat16)).reshape(k // 32, 32, n)
    amax = np.abs(w).max(1)
    byte = np.clip(np.where(amax > 0, np.frexp(amax)[1] - 1 + 127 - 7, 1), 1, 254)
    scaled = (w * np.exp2(127.0 - byte)[:, None, :]).reshape(k, n).astype(np.float32)
    words = np.ascontiguousarray(scaled.reshape(k // 512, 128, 4, n).transpose(0, 1, 3, 2)).astype(ml_dtypes.float8_e4m3fn).view(np.uint8)
    return words, np.ascontiguousarray(byte.astype(np.uint8).reshape(k // 512, 16, n))


def unpack_weight(words, scales):
    g, p, n, _ = words.shape
    vals = np.ascontiguousarray(words).view(ml_dtypes.float8_e4m3fn).astype(np.float64) * np.repeat(np.exp2(scales.astype(np.float64) - 127.0), 8, axis=1)[..., None]
    return vals.transpose(0, 1, 3, 2).reshape(g * 512, n)


def sigmoid(v):
    return 1.0 / (1.0 + np.exp(-np.maximum(v, -700.0)))


K, T, S, N, H, W = 512, 2048, 512, 512, 512, 256


def setup_inputs():
    n = np.random.standard_normal
    s = mx_kscale(K)[:, None]
    u = mx_kscale(S)
    packed_xT = pack_weight(n((K, T)) * s)
    perm = np.stack([np.random.permutation(H) for _ in range(8)])
    return {
        "x_words": packed_xT[0],
        "x_scales": packed_xT[1],
        "wa": (n((K, H)) / np.sqrt(K) / s).astype(np.float32),
        "wb": (n((K, N)) / np.sqrt(K) / s).astype(np.float32),
        "gt": (np.random.uniform(0.5, 1.5, (S, 1)) * u[:, None]).astype(np.float32),
        "gi": (np.random.uniform(0.5, 1.5, (S, 1)) / u[:, None]).astype(np.float32),
        "offs": striped(np.random.permutation(T)[:S]),
        "two": striped(np.random.permutation(T)[:S]),
        "n1": striped8(perm[:, :W]),
        "n2": striped8(perm[:, W:]),
        "n3": striped8(np.stack([np.random.permutation(N) for _ in range(8)])),
        "n4": striped8(np.stack([np.random.permutation(N) for _ in range(8)])),
    }


def reference(x_words, x_scales, wa, wb, gt, gi, offs, two, n1, n2, n3, n4):
    xq = unpack_weight(x_words, x_scales)[:, unstriped(offs)]
    a = xq.T @ mxq(f64(wa), 0, "e4m3")
    pb = a[np.arange(S)[:, None], runs(n2, S)]
    pa = a[np.arange(S)[:, None], runs(n1, S)]
    rb = pb * sigmoid(pb - pa)
    ra = pa * sigmoid(pa - pb)
    ds = np.zeros((S, H))
    ds[np.arange(S)[:, None], runs(n1, S)] = ra
    dt = ds.copy()
    dt[np.arange(S)[:, None], runs(n2, S)] = rb
    z = f64(gt) * dt
    x_two = unpack_weight(x_words, x_scales)[:, unstriped(two)]
    b = x_two.T @ mxq(f64(wb), 0, "e4m3")
    z2 = f64(gi) * b
    cv = 0.0625 * ((mxq(z, 0, "e4m3").T @ mxq(z2, 0, "e4m3")))
    st = np.maximum(cv, cv[np.arange(H)[:, None], runs(n3, H)])
    return np.minimum(st, st[np.arange(H)[:, None], runs(n4, H)])

@@ -1,0 +1,225 @@
+from contextlib import ExitStack
+
+import concourse.mybir as mybir
+
+F32 = mybir.dt.float32
+BF16 = mybir.dt.bfloat16
+I32 = mybir.dt.int32
+U32 = mybir.dt.uint32
+U16 = mybir.dt.uint16
+U8 = mybir.dt.uint8
+FP8X4 = mybir.dt.float8_e4m3fn_x4
+ALU = mybir.AluOpType
+ACT = mybir.ActivationFunctionType
+
+P = 128
+PACK = 4
+T = 2048
+S = 512
+W = 256
+FLOPS = 3 * 2 * 512 * 512 * 512
+
+
+def tile_picked_momduelhopmn_none_p_kernel(
+    tc, x_words, x_scales, wa, wb, gt, gi, offs, two, n1, n2, n3, n4, out
+):
+    nc = tc.nc
+    with ExitStack() as ctx:
+        keep = ctx.enter_context(tc.tile_pool(name="keep", bufs=1))
+        psum = ctx.enter_context(tc.psum_pool(name="psum", bufs=1))
+
+        def sb(name, shape, dtype, tag=None):
+            return keep.tile(shape, dtype, name=name, tag=tag or name, align_bytes=64)
+
+        def load_list(name, src):
+            tile = keep.tile(list(src.shape), U16, name=name)
+            nc.sync.dma_start(tile[:], src)
+            return tile
+
+        xs = sb("xs", [P, T], U8)
+        nc.vector.memset(xs[:].bitcast(I32), 0)
+        warm = sb("warm", [P, 1], F32)
+        warm_out = sb("warm_out", [P, 1], F32)
+        nc.vector.memset(warm[:], 0.0)
+        nc.scalar.activation(warm_out[:], warm[:], ACT.Sigmoid)
+        for q in range(4):
+            nc.sync.dma_start(xs[32 * q : 32 * q + 4, :].bitcast(I32), x_scales[0, 4 * q : 4 * q + 4, :].bitcast(I32))
+        offs_sb = load_list("offs_sb", offs)
+        two_sb = load_list("two_sb", two)
+        wa_raw = sb("wa_raw", [P, PACK, S], F32)
+        nc.sync.dma_start(wa_raw[:], wa.rearrange("(p j) n -> p j n", j=PACK))
+        xw = sb("xw", [P, T], I32)
+        nc.sync.dma_start(xw[:], x_words[0].rearrange("p n t -> p (n t)").bitcast(I32))
+        n1_sb = load_list("n1_sb", n1)
+        n2_sb = load_list("n2_sb", n2)
+        wb_raw = sb("wb_raw", [P, PACK, S], F32)
+        nc.sync.dma_start(wb_raw[:], wb.rearrange("(p j) n -> p j n", j=PACK))
+        gi_sb = sb("gi_sb", [P, PACK], F32)
+        nc.sync.dma_start(gi_sb[:], gi.rearrange("(p j) o -> p (j o)", j=PACK))
+        gt_sb = sb("gt_sb", [P, PACK], F32)
+        nc.sync.dma_start(gt_sb[:], gt.rearrange("(p j) o -> p (j o)", j=PACK))
+        n3_sb = load_list("n3_sb", n3)
+        n4_sb = load_list("n4_sb", n4)
+
+        def interleave(dst, src, c0, c1, copy=nc.scalar.copy):
+            copy(
+                dst[:, PACK * c0 : PACK * c1].rearrange("p (c i j) -> p c j i", i=4, j=PACK),
+                src[:, :, c0:c1].rearrange("p j (c i) -> p c j i", i=4),
+            )
+
+        def quantize(codes, scales, grouped, c0, c1):
+            nc.vector.quantize_mx(
+                out=codes[:, c0:c1].bitcast(FP8X4), scales=scales[:, c0:c1], in_=grouped[:, PACK * c0 : PACK * c1]
+            )
+
+        def pick_bytes(name, lst):
+            picked = sb(name + "_picked", [P, S], U8)
+            nc.vector.tensor_copy(picked[:], xs[:].indirect(lst[:]))
+            dealt = sb(name + "_dealt", [P, S], U8)
+            nc.vector.tensor_copy(
+                dealt[:].rearrange("p (j m) -> p m j", j=PACK), picked[:].rearrange("p (m j) -> p m j", j=PACK)
+            )
+            return dealt
+
+        def pick_words(name, lst, tag=None):
+            dealt = sb(name, [P, S], U32, tag)
+            nc.vector.tensor_copy(dealt[:].rearrange("p (j m) -> p m j", j=PACK), xw[:].bitcast(U32).indirect(lst[:]))
+            return dealt
+
+        def product(bank, codes, scales, j, rhs_codes, rhs_scales):
+            nc.tensor.matmul_mx(
+                out=bank[:],
+                lhsT=codes[:, P * j : P * (j + 1)].bitcast(FP8X4),
+                lhsT_scale=scales[:, P * j : P * (j + 1)],
+                rhs=rhs_codes[:].bitcast(FP8X4),
+                rhs_scale=rhs_scales[:],
+                start=True,
+                stop=True,
+            )
+
+        xa_scales = pick_bytes("xa_scales", offs_sb)
+
+        wa_g = sb("wa_g", [P, PACK * S], BF16)
+        wa_codes = sb("wa_codes", [P, S], U32)
+        wa_scales = sb("wa_scales", [P, S], U8)
+        interleave(wa_g, wa_raw, 0, W)
+        interleave(wa_g, wa_raw, W, S, nc.vector.tensor_copy)
+        quantize(wa_codes, wa_scales, wa_g, W, S)
+        quantize(wa_codes, wa_scales, wa_g, 0, W)
+        xa_codes = pick_words("xa_codes", offs_sb)
+        xb_scales = pick_bytes("xb_scales", two_sb)
+        xb_codes = pick_words("xb_codes", two_sb, "wa_g")
+
+        a_sb = []
+        for j in range(PACK):
+            bank = psum.tile([P, S], F32, name="bank_a%d" % j, tag="lo%d" % j)
+            product(bank, xa_codes, xa_scales, j, wa_codes, wa_scales)
+            a_j = sb("a%d" % j, [P, S], F32)
+            nc.scalar.copy(a_j[:], bank[:])
+            a_sb.append(a_j)
+
+        cv_win = [sb("cv_win%d" % j, [P, 2 * S], F32) for j in range(PACK)]
+        st_win = [sb("st_win%d" % j, [P, 2 * S], F32) for j in range(PACK)]
+        dt = [sb("dt%d" % j, [P, S], F32) for j in range(PACK)]
+        pa = [cv_win[j][:, S : S + W] for j in range(PACK)]
+        pb = [cv_win[j][:, S + W :] for j in range(PACK)]
+        sa = [st_win[j][:, S : S + W] for j in range(PACK)]
+        sbb = [st_win[j][:, S + W :] for j in range(PACK)]
+
+        def fetch_a(j):
+            nc.vector.tensor_copy(pa[j], a_sb[j][:].indirect(n1_sb[:]))
+
+        def fetch_b(j):
+            nc.vector.tensor_copy(pb[j], a_sb[j][:].indirect(n2_sb[:]))
+
+        def duel(j):
+            nc.vector.tensor_tensor(diff[j], pa[j], pb[j], ALU.subtract)
+
+        def gate_a(j):
+            nc.scalar.activation(sa[j], diff[j], ACT.Sigmoid)
+
+        def gate_b(j):
+            nc.scalar.activation(sbb[j], diff[j], ACT.Sigmoid, scale=-1.0)
+
+        def put_a(j):
+            nc.vector.tensor_tensor(dt[j][:].indirect(n1_sb[:]), pa[j], sa[j], ALU.mult)
+
+        def put_b(j):
+            nc.vector.tensor_tensor(dt[j][:].indirect(n2_sb[:]), pb[j], sbb[j], ALU.mult)
+
+        def weigh(j, t0, t1):
+            nc.scalar.activation(
+                z_view[:, t0:t1, :, j],
+                dt[j][:].rearrange("p (m t) -> p t m", t=PACK)[:, t0:t1, :],
+                ACT.Copy,
+                scale=gt_sb[:, j : j + 1],
+            )
+
+        wb_g = sb("wb_g", [P, PACK * S], BF16, "wa_codes")
+        wb_codes = sb("wb_codes", [P, S], U32)
+        wb_scales = sb("wb_scales", [P, S], U8)
+        z2_rows = sb("z2_rows", [P, PACK, S], BF16)
+        z2_g = sb("z2_g", [P, PACK * S], BF16)
+        z2_codes = sb("z2_codes", [P, S], U32)
+        z2_scales = sb("z2_scales", [P, S], U8)
+
+        for j in range(PACK):
+            fetch_a(j)
+            fetch_b(j)
+        interleave(wb_g, wb_raw, 0, S)
+        diffs = sb("diffs", [P, PACK * W], F32, "wb_raw")
+        diff = [diffs[:, W * j : W * (j + 1)] for j in range(PACK)]
+        for j in range(PACK):
+            duel(j)
+        quantize(wb_codes, wb_scales, wb_g, 0, S)
+        for h in range(2):
+            pair = (2 * h, 2 * h + 1)
+            for j in pair:
+                gate_a(j)
+                put_a(j)
+            for j in pair:
+                gate_b(j)
+                put_b(j)
+        for j in range(PACK):
+            bank = psum.tile([P, S], F32, name="bank_b%d" % j, tag="hi%d" % j)
+            product(bank, xb_codes, xb_scales, j, wb_codes, wb_scales)
+            nc.scalar.activation(z2_rows[:, j, :], bank[:], ACT.Copy, scale=gi_sb[:, j : j + 1])
+        interleave(z2_g, z2_rows, 0, S)
+        z_g = sb("z_g", [P, PACK * S], BF16, "z2_rows")
+        z_view = z_g[:].rearrange("p (t m j) -> p t m j", t=PACK, j=PACK)
+        for j in range(PACK - 1):
+            weigh(j, 0, PACK)
+        quantize(z2_codes, z2_scales, z2_g, 0, S)
+
+        z_codes = sb("z_codes", [P, S], U32)
+        z_scales = sb("z_scales", [P, S], U8)
+        for t in range(PACK):
+            weigh(3, t, t + 1)
+            quantize(z_codes, z_scales, z_g, P * t, P * (t + 1))
+        for t in range(PACK):
+            bank = psum.tile([P, S], F32, name="bank_c%d" % t, tag="lo%d" % t)
+            product(bank, z_codes, z_scales, t, z2_codes, z2_scales)
+            nc.scalar.activation(cv_win[t][:, :S], bank[:], ACT.Copy, scale=0.0625)
+
+        hop3 = [sb("hop3_%d" % t, [P, S], F32) for t in range(PACK)]
+        hop4 = [sb("hop4_%d" % t, [P, S], F32) for t in range(PACK)]
+        res = [sb("res%d" % t, [P, S], F32) for t in range(PACK)]
+        out_rows = out.rearrange("(m t) n -> t m n", t=PACK)
+
+        def fetch3(t):
+            nc.vector.tensor_copy(hop3[t][:], cv_win[t][:].indirect(n3_sb[:]))
+
+        def larger(t):
+            nc.vector.tensor_tensor(st_win[t][:, :S], cv_win[t][:, :S], hop3[t][:], ALU.max)
+
+        def fetch4(t):
+            nc.vector.tensor_copy(hop4[t][:], st_win[t][:].indirect(n4_sb[:]))
+
+        def smaller(t):
+            nc.vector.tensor_tensor(res[t][:], st_win[t][:, :S], hop4[t][:], ALU.min)
+            nc.sync.dma_start(out_rows[t], res[t][:])
+
+        for t0 in (0, 2):
+            for step in (fetch3, larger, fetch4, smaller):
+                step(t0)
+                step(t0 + 1)

@@ -17,6 +17,7 @@ PACK = 4
 T = 2048
 S = 512
 W = 256
+RUN = 8
 FLOPS = 3 * 2 * 512 * 512 * 512
 
 
@@ -55,9 +56,12 @@ def tile_picked_momduelhopmn_none_p_kernel(
         wb_raw = sb("wb_raw", [P, PACK, S], F32)
         nc.sync.dma_start(wb_raw[:], wb.rearrange("(p j) n -> p j n", j=PACK))
         gi_sb = sb("gi_sb", [P, PACK], F32)
-        nc.sync.dma_start(gi_sb[:], gi.rearrange("(p j) o -> p (j o)", j=PACK))
         gt_sb = sb("gt_sb", [P, PACK], F32)
-        nc.sync.dma_start(gt_sb[:], gt.rearrange("(p j) o -> p (j o)", j=PACK))
+        with nc.allow_non_contiguous_dma(reason="one weight a place"):
+            for tile, src in ((gi_sb, gi), (gt_sb, gt)):
+                by_e = src.rearrange("(b j e) o -> e b (j o)", j=PACK, e=RUN)
+                for e in range(RUN):
+                    nc.sync.dma_start(tile[e:P:RUN, :], by_e[e])
         n3_sb = load_list("n3_sb", n3)
         n4_sb = load_list("n4_sb", n4)
 
@@ -77,22 +81,23 @@ def tile_picked_momduelhopmn_none_p_kernel(
             nc.vector.tensor_copy(picked[:], xs[:].indirect(lst[:]))
             dealt = sb(name + "_dealt", [P, S], U8)
             nc.vector.tensor_copy(
-                dealt[:].rearrange("p (j m) -> p m j", j=PACK), picked[:].rearrange("p (m j) -> p m j", j=PACK)
+                dealt[:].bitcast(I32).rearrange("p (j b w) -> p b j w", j=PACK, w=RUN // 4),
+                picked[:].bitcast(I32).rearrange("p (b j w) -> p b j w", j=PACK, w=RUN // 4),
             )
             return dealt
 
         def pick_words(name, lst, tag=None):
             dealt = sb(name, [P, S], U32, tag)
-            nc.vector.tensor_copy(dealt[:].rearrange("p (j m) -> p m j", j=PACK), xw[:].bitcast(U32).indirect(lst[:]))
+            nc.vector.tensor_copy(dealt[:].rearrange("p (j b e) -> p b j e", j=PACK, e=RUN), xw[:].bitcast(U32).indirect(lst[:]))
             return dealt
 
-        def product(bank, codes, scales, j, rhs_codes, rhs_scales):
+        def product(bank, codes, scales, j, rhs_codes, rhs_scales, c0=0, c1=S):
             nc.tensor.matmul_mx(
-                out=bank[:],
+                out=bank[:, : c1 - c0],
                 lhsT=codes[:, P * j : P * (j + 1)].bitcast(FP8X4),
                 lhsT_scale=scales[:, P * j : P * (j + 1)],
-                rhs=rhs_codes[:].bitcast(FP8X4),
-                rhs_scale=rhs_scales[:],
+                rhs=rhs_codes[:, c0:c1].bitcast(FP8X4),
+                rhs_scale=rhs_scales[:, c0:c1],
                 start=True,
                 stop=True,
             )
@@ -196,7 +201,11 @@ def tile_picked_momduelhopmn_none_p_kernel(
         for t in range(PACK):
             weigh(3, t, t + 1)
             quantize(z_codes, z_scales, z_g, P * t, P * (t + 1))
-        for t in range(PACK):
+        for h in range(2):
+            bank = psum.tile([P, S], F32, name="bank_h%d" % h, tag="hi%d" % h)
+            product(bank, z_codes, z_scales, 0, z2_codes, z2_scales, W * h, W * (h + 1))
+            nc.vector.tensor_scalar(cv_win[0][:, W * h : W * (h + 1)], bank[:, :W], 0.0625, None, ALU.mult)
+        for t in range(1, PACK):
             bank = psum.tile([P, S], F32, name="bank_c%d" % t, tag="lo%d" % t)
             product(bank, z_codes, z_scales, t, z2_codes, z2_scales)
             nc.scalar.activation(cv_win[t][:, :S], bank[:], ACT.Copy, scale=0.0625)
@@ -212,14 +221,28 @@ def tile_picked_momduelhopmn_none_p_kernel(
         def larger(t):
             nc.vector.tensor_tensor(st_win[t][:, :S], cv_win[t][:, :S], hop3[t][:], ALU.max)
 
-        def fetch4(t):
-            nc.vector.tensor_copy(hop4[t][:], st_win[t][:].indirect(n4_sb[:]))
+        def fetch4(t, c0=0, c1=S):
+            nc.vector.tensor_copy(hop4[t][:, c0:c1], st_win[t][:].indirect(n4_sb[:, c0 // 16 : c1 // 16]))
 
-        def smaller(t):
-            nc.vector.tensor_tensor(res[t][:], st_win[t][:, :S], hop4[t][:], ALU.min)
-            nc.sync.dma_start(out_rows[t], res[t][:])
+        def smaller(t, c0=0, c1=S):
+            nc.vector.tensor_tensor(res[t][:, c0:c1], st_win[t][:, c0:c1], hop4[t][:, c0:c1], ALU.min)
+            nc.sync.dma_start(out_rows[t][:, c0:c1], res[t][:, c0:c1])
 
-        for t0 in (0, 2):
-            for step in (fetch3, larger, fetch4, smaller):
-                step(t0)
-                step(t0 + 1)
+        fetch3(0)
+        fetch3(1)
+        larger(0)
+        fetch3(2)
+        larger(1)
+        fetch4(0)
+        fetch3(3)
+        larger(2)
+        smaller(0)
+        fetch4(1)
+        larger(3)
+        fetch4(2)
+        smaller(1)
+        fetch4(3, 0, W)
+        smaller(2)
+        fetch4(3, W, S)
+        smaller(3, 0, W)
+        smaller(3, W, S)

@@ -128,8 +128,7 @@ def tile_picked_momduelhopmn_none_p_kernel(
         dt = [sb("dt%d" % j, [P, S], F32) for j in range(PACK)]
         pa = [cv_win[j][:, S : S + W] for j in range(PACK)]
         pb = [cv_win[j][:, S + W :] for j in range(PACK)]
-        sa = [st_win[j][:, S : S + W] for j in range(PACK)]
-        sbb = [st_win[j][:, S + W :] for j in range(PACK)]
+        diff = [sb("diff%d" % j, [P, W], F32) for j in range(PACK)]
 
         def fetch_a(j):
             nc.vector.tensor_copy(pa[j], a_sb[j][:].indirect(n1_sb[:]))
@@ -138,13 +137,14 @@ def tile_picked_momduelhopmn_none_p_kernel(
             nc.vector.tensor_copy(pb[j], a_sb[j][:].indirect(n2_sb[:]))
 
         def duel(j):
-            nc.vector.tensor_tensor(diff[j], pa[j], pb[j], ALU.subtract)
+            engine = nc.vector if j == PACK - 1 else nc.gpsimd
+            engine.tensor_tensor(diff[j][:], pa[j], pb[j], ALU.subtract)
 
         def gate_a(j):
-            nc.scalar.activation(sa[j], diff[j], ACT.Sigmoid)
+            nc.scalar.activation(sa[j], diff[j][:], ACT.Sigmoid)
 
         def gate_b(j):
-            nc.scalar.activation(sbb[j], diff[j], ACT.Sigmoid, scale=-1.0)
+            nc.scalar.activation(sbb[j], diff[j][:], ACT.Sigmoid, scale=-1.0)
 
         def put_a(j):
             nc.vector.tensor_tensor(dt[j][:].indirect(n1_sb[:]), pa[j], sa[j], ALU.mult)
@@ -171,11 +171,11 @@ def tile_picked_momduelhopmn_none_p_kernel(
         for j in range(PACK):
             fetch_a(j)
             fetch_b(j)
-        interleave(wb_g, wb_raw, 0, S)
-        diffs = sb("diffs", [P, PACK * W], F32, "wb_raw")
-        diff = [diffs[:, W * j : W * (j + 1)] for j in range(PACK)]
-        for j in range(PACK):
             duel(j)
+        interleave(wb_g, wb_raw, 0, S)
+        gates = sb("gates", [P, PACK * S], F32, "wb_raw")
+        sa = [gates[:, S * j : S * j + W] for j in range(PACK)]
+        sbb = [gates[:, S * j + W : S * (j + 1)] for j in range(PACK)]
         quantize(wb_codes, wb_scales, wb_g, 0, S)
         for h in range(2):
             pair = (2 * h, 2 * h + 1)
@@ -210,16 +210,16 @@ def tile_picked_momduelhopmn_none_p_kernel(
             product(bank, z_codes, z_scales, t, z2_codes, z2_scales)
             nc.scalar.activation(cv_win[t][:, :S], bank[:], ACT.Copy, scale=0.0625)
 
-        hop3 = [sb("hop3_%d" % t, [P, S], F32) for t in range(PACK)]
+        hop3 = [st_win[t][:, S:] for t in range(PACK)]
         hop4 = [sb("hop4_%d" % t, [P, S], F32) for t in range(PACK)]
         res = [sb("res%d" % t, [P, S], F32) for t in range(PACK)]
         out_rows = out.rearrange("(m t) n -> t m n", t=PACK)
 
         def fetch3(t):
-            nc.vector.tensor_copy(hop3[t][:], cv_win[t][:].indirect(n3_sb[:]))
+            nc.vector.tensor_copy(hop3[t], cv_win[t][:].indirect(n3_sb[:]))
 
         def larger(t):
-            nc.vector.tensor_tensor(st_win[t][:, :S], cv_win[t][:, :S], hop3[t][:], ALU.max)
+            nc.vector.tensor_tensor(st_win[t][:, :S], cv_win[t][:, :S], hop3[t], ALU.max)
 
         def fetch4(t, c0=0, c1=S):
             nc.vector.tensor_copy(hop4[t][:, c0:c1], st_win[t][:].indirect(n4_sb[:, c0 // 16 : c1 // 16]))

@@ -201,48 +201,63 @@ def tile_picked_momduelhopmn_none_p_kernel(
         for t in range(PACK):
             weigh(3, t, t + 1)
             quantize(z_codes, z_scales, z_g, P * t, P * (t + 1))
+        cv_banks = [[], [], [], []]
         for h in range(2):
             bank = psum.tile([P, S], F32, name="bank_h%d" % h, tag="hi%d" % h)
+            cv_banks[0].append((bank, W * h, W * (h + 1)))
             product(bank, z_codes, z_scales, 0, z2_codes, z2_scales, W * h, W * (h + 1))
             nc.vector.tensor_scalar(cv_win[0][:, W * h : W * (h + 1)], bank[:, :W], 0.0625, None, ALU.mult)
         for t in range(1, PACK):
             bank = psum.tile([P, S], F32, name="bank_c%d" % t, tag="lo%d" % t)
+            cv_banks[t].append((bank, 0, S))
             product(bank, z_codes, z_scales, t, z2_codes, z2_scales)
             nc.scalar.activation(cv_win[t][:, :S], bank[:], ACT.Copy, scale=0.0625)
 
         hop3 = [st_win[t][:, S:] for t in range(PACK)]
         hop4 = [sb("hop4_%d" % t, [P, S], F32) for t in range(PACK)]
-        res = [sb("res%d" % t, [P, S], F32) for t in range(PACK)]
         out_rows = out.rearrange("(m t) n -> t m n", t=PACK)
 
         def fetch3(t):
             nc.vector.tensor_copy(hop3[t], cv_win[t][:].indirect(n3_sb[:]))
 
         def larger(t):
-            nc.vector.tensor_tensor(st_win[t][:, :S], cv_win[t][:, :S], hop3[t], ALU.max)
+            for bank, c0, c1 in cv_banks[t]:
+                nc.vector.scalar_tensor_tensor(
+                    st_win[t][:, c0:c1], bank[:, : c1 - c0], 0.0625, hop3[t][:, c0:c1], ALU.mult, ALU.max
+                )
+
+        def by_excess(name, dst, base, hi, lo, op):
+            gap = sb(name + "_gap", [P, S], F32)
+            excess = sb(name + "_excess", [P, S], F32)
+            nc.gpsimd.tensor_tensor(gap[:], hi, lo, ALU.subtract)
+            nc.scalar.activation(excess[:], gap[:], ACT.Relu)
+            nc.gpsimd.tensor_tensor(dst, base, excess[:], op)
 
         def fetch4(t, c0=0, c1=S):
             nc.vector.tensor_copy(hop4[t][:, c0:c1], st_win[t][:].indirect(n4_sb[:, c0 // 16 : c1 // 16]))
 
         def smaller(t, c0=0, c1=S):
-            nc.vector.tensor_tensor(res[t][:, c0:c1], st_win[t][:, c0:c1], hop4[t][:, c0:c1], ALU.min)
-            nc.sync.dma_start(out_rows[t][:, c0:c1], res[t][:, c0:c1])
+            res = rest[:, S * (t - 1) + c0 : S * (t - 1) + c1]
+            nc.vector.tensor_tensor(res, st_win[t][:, c0:c1], hop4[t][:, c0:c1], ALU.min)
+            nc.sync.dma_start(out_rows[t][:, c0:c1], res)
 
         fetch3(0)
         fetch3(1)
+        by_excess("max1", st_win[1][:, :S], cv_win[1][:, :S], hop3[1], cv_win[1][:, :S], ALU.add)
         larger(0)
         fetch3(2)
-        larger(1)
         fetch4(0)
-        fetch3(3)
+        res0 = sb("res0", [P, S], F32)
+        by_excess("min0", res0[:], st_win[0][:, :S], st_win[0][:, :S], hop4[0][:], ALU.subtract)
+        nc.sync.dma_start(out_rows[0], res0[:])
         larger(2)
-        smaller(0)
-        fetch4(1)
-        larger(3)
+        fetch3(3)
         fetch4(2)
-        smaller(1)
-        fetch4(3, 0, W)
+        larger(3)
+        fetch4(3)
+        fetch4(1)
+        rest = sb("rest", [P, 3 * S], F32, "min0_excess")
         smaller(2)
-        fetch4(3, W, S)
-        smaller(3, 0, W)
-        smaller(3, W, S)
+        smaller(3)
+        smaller(1, 0, W)
+        smaller(1, W, S)

from contextlib import ExitStack

import concourse.mybir as mybir

F32 = mybir.dt.float32
BF16 = mybir.dt.bfloat16
I32 = mybir.dt.int32
U32 = mybir.dt.uint32
U16 = mybir.dt.uint16
U8 = mybir.dt.uint8
FP8X4 = mybir.dt.float8_e4m3fn_x4
ALU = mybir.AluOpType
ACT = mybir.ActivationFunctionType

P = 128
PACK = 4
T = 2048
S = 512
W = 256
RUN = 8
FLOPS = 3 * 2 * 512 * 512 * 512


def tile_picked_momduelhopmn_none_p_kernel(
    tc, x_words, x_scales, wa, wb, gt, gi, offs, two, n1, n2, n3, n4, out
):
    nc = tc.nc
    with ExitStack() as ctx:
        keep = ctx.enter_context(tc.tile_pool(name="keep", bufs=1))
        psum = ctx.enter_context(tc.psum_pool(name="psum", bufs=1))

        def sb(name, shape, dtype, tag=None):
            return keep.tile(shape, dtype, name=name, tag=tag or name, align_bytes=64)

        def load_list(name, src):
            tile = keep.tile(list(src.shape), U16, name=name)
            nc.sync.dma_start(tile[:], src)
            return tile

        xs = sb("xs", [P, T], U8)
        nc.vector.memset(xs[:].bitcast(I32), 0)
        warm = sb("warm", [P, 1], F32)
        warm_out = sb("warm_out", [P, 1], F32)
        nc.vector.memset(warm[:], 0.0)
        nc.scalar.activation(warm_out[:], warm[:], ACT.Sigmoid)
        for q in range(4):
            nc.sync.dma_start(xs[32 * q : 32 * q + 4, :].bitcast(I32), x_scales[0, 4 * q : 4 * q + 4, :].bitcast(I32))
        offs_sb = load_list("offs_sb", offs)
        two_sb = load_list("two_sb", two)
        wa_raw = sb("wa_raw", [P, PACK, S], F32)
        nc.sync.dma_start(wa_raw[:], wa.rearrange("(p j) n -> p j n", j=PACK))
        xw = sb("xw", [P, T], I32)
        nc.sync.dma_start(xw[:], x_words[0].rearrange("p n t -> p (n t)").bitcast(I32))
        n1_sb = load_list("n1_sb", n1)
        n2_sb = load_list("n2_sb", n2)
        wb_raw = sb("wb_raw", [P, PACK, S], F32)
        nc.sync.dma_start(wb_raw[:], wb.rearrange("(p j) n -> p j n", j=PACK))
        gi_sb = sb("gi_sb", [P, PACK], F32)
        gt_sb = sb("gt_sb", [P, PACK], F32)
        with nc.allow_non_contiguous_dma(reason="one weight a place"):
            for tile, src in ((gi_sb, gi), (gt_sb, gt)):
                by_e = src.rearrange("(b j e) o -> e b (j o)", j=PACK, e=RUN)
                for e in range(RUN):
                    nc.sync.dma_start(tile[e:P:RUN, :], by_e[e])
        n3_sb = load_list("n3_sb", n3)
        n4_sb = load_list("n4_sb", n4)

        def interleave(dst, src, c0, c1, copy=nc.scalar.copy):
            copy(
                dst[:, PACK * c0 : PACK * c1].rearrange("p (c i j) -> p c j i", i=4, j=PACK),
                src[:, :, c0:c1].rearrange("p j (c i) -> p c j i", i=4),
            )

        def quantize(codes, scales, grouped, c0, c1):
            nc.vector.quantize_mx(
                out=codes[:, c0:c1].bitcast(FP8X4), scales=scales[:, c0:c1], in_=grouped[:, PACK * c0 : PACK * c1]
            )

        def pick_bytes(name, lst):
            picked = sb(name + "_picked", [P, S], U8)
            nc.vector.tensor_copy(picked[:], xs[:].indirect(lst[:]))
            dealt = sb(name + "_dealt", [P, S], U8)
            nc.vector.tensor_copy(
                dealt[:].bitcast(I32).rearrange("p (j b w) -> p b j w", j=PACK, w=RUN // 4),
                picked[:].bitcast(I32).rearrange("p (b j w) -> p b j w", j=PACK, w=RUN // 4),
            )
            return dealt

        def pick_words(name, lst, tag=None):
            dealt = sb(name, [P, S], U32, tag)
            nc.vector.tensor_copy(dealt[:].rearrange("p (j b e) -> p b j e", j=PACK, e=RUN), xw[:].bitcast(U32).indirect(lst[:]))
            return dealt

        def product(bank, codes, scales, j, rhs_codes, rhs_scales, c0=0, c1=S):
            nc.tensor.matmul_mx(
                out=bank[:, : c1 - c0],
                lhsT=codes[:, P * j : P * (j + 1)].bitcast(FP8X4),
                lhsT_scale=scales[:, P * j : P * (j + 1)],
                rhs=rhs_codes[:, c0:c1].bitcast(FP8X4),
                rhs_scale=rhs_scales[:, c0:c1],
                start=True,
                stop=True,
            )

        xa_scales = pick_bytes("xa_scales", offs_sb)

        wa_g = sb("wa_g", [P, PACK * S], BF16)
        wa_codes = sb("wa_codes", [P, S], U32)
        wa_scales = sb("wa_scales", [P, S], U8)
        interleave(wa_g, wa_raw, 0, W)
        interleave(wa_g, wa_raw, W, S, nc.vector.tensor_copy)
        quantize(wa_codes, wa_scales, wa_g, W, S)
        quantize(wa_codes, wa_scales, wa_g, 0, W)
        xa_codes = pick_words("xa_codes", offs_sb)
        xb_scales = pick_bytes("xb_scales", two_sb)
        xb_codes = pick_words("xb_codes", two_sb, "wa_g")

        a_sb = []
        for j in range(PACK):
            bank = psum.tile([P, S], F32, name="bank_a%d" % j, tag="lo%d" % j)
            product(bank, xa_codes, xa_scales, j, wa_codes, wa_scales)
            a_j = sb("a%d" % j, [P, S], F32)
            nc.scalar.copy(a_j[:], bank[:])
            a_sb.append(a_j)

        cv_win = [sb("cv_win%d" % j, [P, 2 * S], F32) for j in range(PACK)]
        st_win = [sb("st_win%d" % j, [P, 2 * S], F32) for j in range(PACK)]
        dt = [sb("dt%d" % j, [P, S], F32) for j in range(PACK)]
        pa = [cv_win[j][:, S : S + W] for j in range(PACK)]
        pb = [cv_win[j][:, S + W :] for j in range(PACK)]
        diff = [sb("diff%d" % j, [P, W], F32) for j in range(PACK)]

        def fetch_a(j):
            nc.vector.tensor_copy(pa[j], a_sb[j][:].indirect(n1_sb[:]))

        def fetch_b(j):
            nc.vector.tensor_copy(pb[j], a_sb[j][:].indirect(n2_sb[:]))

        def duel(j):
            engine = nc.vector if j == PACK - 1 else nc.gpsimd
            engine.tensor_tensor(diff[j][:], pa[j], pb[j], ALU.subtract)

        def gate_a(j):
            nc.scalar.activation(sa[j], diff[j][:], ACT.Sigmoid)

        def gate_b(j):
            nc.scalar.activation(sbb[j], diff[j][:], ACT.Sigmoid, scale=-1.0)

        def put_a(j):
            nc.vector.tensor_tensor(dt[j][:].indirect(n1_sb[:]), pa[j], sa[j], ALU.mult)

        def put_b(j):
            nc.vector.tensor_tensor(dt[j][:].indirect(n2_sb[:]), pb[j], sbb[j], ALU.mult)

        def weigh(j, t0, t1):
            nc.scalar.activation(
                z_view[:, t0:t1, :, j],
                dt[j][:].rearrange("p (m t) -> p t m", t=PACK)[:, t0:t1, :],
                ACT.Copy,
                scale=gt_sb[:, j : j + 1],
            )

        wb_g = sb("wb_g", [P, PACK * S], BF16, "wa_codes")
        wb_codes = sb("wb_codes", [P, S], U32)
        wb_scales = sb("wb_scales", [P, S], U8)
        z2_rows = sb("z2_rows", [P, PACK, S], BF16)
        z2_g = sb("z2_g", [P, PACK * S], BF16)
        z2_codes = sb("z2_codes", [P, S], U32)
        z2_scales = sb("z2_scales", [P, S], U8)

        for j in range(PACK):
            fetch_a(j)
            fetch_b(j)
            duel(j)
        interleave(wb_g, wb_raw, 0, S)
        gates = sb("gates", [P, PACK * S], F32, "wb_raw")
        sa = [gates[:, S * j : S * j + W] for j in range(PACK)]
        sbb = [gates[:, S * j + W : S * (j + 1)] for j in range(PACK)]
        quantize(wb_codes, wb_scales, wb_g, 0, S)
        for h in range(2):
            pair = (2 * h, 2 * h + 1)
            for j in pair:
                gate_a(j)
                put_a(j)
            for j in pair:
                gate_b(j)
                put_b(j)
        for j in range(PACK):
            bank = psum.tile([P, S], F32, name="bank_b%d" % j, tag="hi%d" % j)
            product(bank, xb_codes, xb_scales, j, wb_codes, wb_scales)
            nc.scalar.activation(z2_rows[:, j, :], bank[:], ACT.Copy, scale=gi_sb[:, j : j + 1])
        interleave(z2_g, z2_rows, 0, S)
        z_g = sb("z_g", [P, PACK * S], BF16, "z2_rows")
        z_view = z_g[:].rearrange("p (t m j) -> p t m j", t=PACK, j=PACK)
        for j in range(PACK - 1):
            weigh(j, 0, PACK)
        quantize(z2_codes, z2_scales, z2_g, 0, S)

        z_codes = sb("z_codes", [P, S], U32)
        z_scales = sb("z_scales", [P, S], U8)
        for t in range(PACK):
            weigh(3, t, t + 1)
            quantize(z_codes, z_scales, z_g, P * t, P * (t + 1))
        cv_banks = [[], [], [], []]
        for h in range(2):
            bank = psum.tile([P, S], F32, name="bank_h%d" % h, tag="hi%d" % h)
            cv_banks[0].append((bank, W * h, W * (h + 1)))
            product(bank, z_codes, z_scales, 0, z2_codes, z2_scales, W * h, W * (h + 1))
            nc.vector.tensor_scalar(cv_win[0][:, W * h : W * (h + 1)], bank[:, :W], 0.0625, None, ALU.mult)
        for t in range(1, PACK):
            bank = psum.tile([P, S], F32, name="bank_c%d" % t, tag="lo%d" % t)
            cv_banks[t].append((bank, 0, S))
            product(bank, z_codes, z_scales, t, z2_codes, z2_scales)
            nc.scalar.activation(cv_win[t][:, :S], bank[:], ACT.Copy, scale=0.0625)

        hop3 = [st_win[t][:, S:] for t in range(PACK)]
        hop4 = [sb("hop4_%d" % t, [P, S], F32) for t in range(PACK)]
        out_rows = out.rearrange("(m t) n -> t m n", t=PACK)

        def fetch3(t):
            nc.vector.tensor_copy(hop3[t], cv_win[t][:].indirect(n3_sb[:]))

        def larger(t):
            for bank, c0, c1 in cv_banks[t]:
                nc.vector.scalar_tensor_tensor(
                    st_win[t][:, c0:c1], bank[:, : c1 - c0], 0.0625, hop3[t][:, c0:c1], ALU.mult, ALU.max
                )

        def by_excess(name, dst, base, hi, lo, op):
            gap = sb(name + "_gap", [P, S], F32)
            excess = sb(name + "_excess", [P, S], F32)
            nc.gpsimd.tensor_tensor(gap[:], hi, lo, ALU.subtract)
            nc.scalar.activation(excess[:], gap[:], ACT.Relu)
            nc.gpsimd.tensor_tensor(dst, base, excess[:], op)

        def fetch4(t, c0=0, c1=S):
            nc.vector.tensor_copy(hop4[t][:, c0:c1], st_win[t][:].indirect(n4_sb[:, c0 // 16 : c1 // 16]))

        def smaller(t, c0=0, c1=S):
            res = rest[:, S * (t - 1) + c0 : S * (t - 1) + c1]
            nc.vector.tensor_tensor(res, st_win[t][:, c0:c1], hop4[t][:, c0:c1], ALU.min)
            nc.sync.dma_start(out_rows[t][:, c0:c1], res)

        fetch3(0)
        fetch3(1)
        by_excess("max1", st_win[1][:, :S], cv_win[1][:, :S], hop3[1], cv_win[1][:, :S], ALU.add)
        larger(0)
        fetch3(2)
        fetch4(0)
        res0 = sb("res0", [P, S], F32)
        by_excess("min0", res0[:], st_win[0][:, :S], st_win[0][:, :S], hop4[0][:], ALU.subtract)
        nc.sync.dma_start(out_rows[0], res0[:])
        larger(2)
        fetch3(3)
        fetch4(2)
        larger(3)
        fetch4(3)
        fetch4(1)
        rest = sb("rest", [P, 3 * S], F32, "min0_excess")
        smaller(2)
        smaller(3)
        smaller(1, 0, W)
        smaller(1, W, S)
